import numpy as np
import ml_dtypes


def mxq(x, axis, fmt="e4m3"):
    dtype, down = {"e4m3": (ml_dtypes.float8_e4m3fn, 7), "e5m2": (ml_dtypes.float8_e5m2, 14)}[fmt]
    v = np.moveaxis(np.asarray(x, np.float32).astype(ml_dtypes.bfloat16).astype(np.float64), axis, -1)
    blocks = v.reshape(v.shape[:-1] + (-1, 32))
    amax = np.abs(blocks).max(-1, keepdims=True)
    byte = np.maximum(np.where(amax > 0, np.frexp(amax)[1] - 1 + 127, 0) - down, 1)
    scale = np.exp2(byte - 127.0)
    codes = (blocks / scale).astype(np.float32).astype(dtype).astype(np.float64)
    return np.moveaxis((codes * scale).reshape(v.shape), -1, axis)


WIDE = False


def mx_kscale(k):
    if not WIDE:
        return np.ones(k)
    levels = np.array([10, -10, 5, -5, 0])
    if k % 512:
        return np.exp2(np.random.permutation(np.resize(levels, k // 32))).repeat(32)
    a = np.empty((k // 512, 16))
    for p in range(k // 512):
        a[p, :8] = np.random.permutation(np.resize(levels, 8))
        for g in range(8):
            far = levels[np.abs(levels - a[p, g]) >= 10]
            a[p, g + 8] = far[np.random.randint(len(far))]
    return np.exp2(a.ravel()).repeat(32)


def f64(x):
    return np.asarray(x).astype(np.float64)


def striped(idx):
    return np.tile(idx.reshape(-1, 16).T, (8, 1)).astype(np.uint16)


def unstriped(offs):
    return offs[:16].T.reshape(-1).astype(np.int64)


def pack_weight(w):
    k, n = w.shape
    w = f64(np.asarray(w, np.float32).astype(ml_dtypes.bfloat16)).reshape(k // 32, 32, n)
    amax = np.abs(w).max(1)
    byte = np.clip(np.where(amax > 0, np.frexp(amax)[1] - 1 + 127 - 7, 1), 1, 254)
    scaled = (w * np.exp2(127.0 - byte)[:, None, :]).reshape(k, n).astype(np.float32)
    words = np.ascontiguousarray(scaled.reshape(k // 512, 128, 4, n).transpose(0, 1, 3, 2)).astype(ml_dtypes.float8_e4m3fn).view(np.uint8)
    return words, np.ascontiguousarray(byte.astype(np.uint8).reshape(k // 512, 16, n))


def unpack_weight(words, scales):
    g, p, n, _ = words.shape
    vals = np.ascontiguousarray(words).view(ml_dtypes.float8_e4m3fn).astype(np.float64) * np.repeat(np.exp2(scales.astype(np.float64) - 127.0), 8, axis=1)[..., None]
    return vals.transpose(0, 1, 3, 2).reshape(g * 512, n)


def sigmoid(v):
    return 1.0 / (1.0 + np.exp(-np.maximum(v, -700.0)))


K, T, S, V = 1024, 2048, 512, 256


def setup_inputs():
    n = np.random.standard_normal
    s = mx_kscale(K)[:, None]
    packed_xT = pack_weight(n((K, T)) * s)
    return {
        "x_words": packed_xT[0],
        "x_scales": packed_xT[1],
        "hT": (n((K, V)) / np.sqrt(K) / s).astype(np.float32),
        "offs": striped(np.random.permutation(T)[:S]),
    }


def reference(x_words, x_scales, hT, offs):
    hTq = mxq(f64(hT), 0, "e4m3")
    xq = unpack_weight(x_words, x_scales)[:, unstriped(offs)]
    y = hTq.T @ xq
    ex = np.exp(y - y.max(axis=1, keepdims=True))
    pr = 100.0 * (ex / ex.sum(axis=1, keepdims=True))
    sm = np.maximum(np.maximum(np.pad(pr, ((0, 0), (1, 0)))[:, :S], pr), np.pad(pr, ((0, 0), (0, 1)))[:, 1:])
    mean = sm.mean(axis=1, keepdims=True)
    return pr * (sigmoid(4.0 * (sm - (1.5 * mean)))) + 0.2 * sm

@@ -1,0 +1,155 @@
+from contextlib import ExitStack
+
+import concourse.mybir as mybir
+
+K, T, S, V = 1024, 2048, 512, 256
+FLOPS = 2 * K * S * V
+
+F32 = mybir.dt.float32
+BF16 = mybir.dt.bfloat16
+I32 = mybir.dt.int32
+U32 = mybir.dt.uint32
+U16 = mybir.dt.uint16
+U8 = mybir.dt.uint8
+FP8X4 = mybir.dt.float8_e4m3fn_x4
+ALU = mybir.AluOpType
+ACT = mybir.ActivationFunctionType
+AX = mybir.AxisListType
+
+P = 128
+PACK = 4
+K_PASS = P * PACK
+PASSES = K // K_PASS
+TILES = V // P
+PAD = 4
+
+
+def tile_picked_ysnapv_max_p_kernel(tc, x_words, x_scales, hT, offs, out):
+    nc = tc.nc
+    with ExitStack() as ctx:
+        keep = ctx.enter_context(tc.tile_pool(name="keep", bufs=1))
+        psum = ctx.enter_context(tc.psum_pool(name="psum", bufs=1))
+
+        offsets = keep.tile([P, S // 16], U16, name="offsets")
+        scale_table = keep.tile([P, T], U8, name="scale_table", tag="chain_a", align_bytes=64)
+        nc.vector.memset(scale_table[:].bitcast(I32), 0)
+        for q in range(4):
+            nc.scalar.dma_start(
+                scale_table[32 * q : 32 * q + 4 * PASSES, :].bitcast(I32),
+                x_scales[:, 4 * q : 4 * q + 4, :].bitcast(I32),
+            )
+
+        word_table = [
+            keep.tile([P, T], I32, name="word_table0", align_bytes=64),
+            keep.tile([P, T], I32, name="word_table1", tag="chain_c", align_bytes=64),
+        ]
+        h_raw = [keep.tile([P, PACK, V], F32, name=f"h_raw{g}", align_bytes=64) for g in range(PASSES)]
+        for g in range(PASSES):
+            nc.sync.dma_start(word_table[g][:], x_words[g].rearrange("p n t -> p (n t)").bitcast(I32))
+            if g == 0:
+                nc.sync.dma_start(offsets[:], offs)
+            nc.sync.dma_start(h_raw[g][:], hT[g * K_PASS : (g + 1) * K_PASS, :].rearrange("(p j) w -> p j w", j=PACK))
+
+        consts = keep.tile([P, 4], F32, name="consts")
+        for i, c in enumerate((50.0, 200.0, -300.0 / S, 20.0)):
+            nc.vector.memset(consts[:, i : i + 1], c)
+        e = [keep.tile([P, S + 2 * PAD], F32, name=f"e{t}", align_bytes=64) for t in range(TILES)]
+        for t in range(TILES):
+            nc.vector.memset(e[t][:, PAD - 1 : PAD], 0.0)
+            nc.vector.memset(e[t][:, PAD + S : PAD + S + 1], 0.0)
+
+        key_scales = keep.tile([P, S], U8, name="key_scales", align_bytes=64)
+        acc = [psum.tile([P, S], F32, name=f"acc{t}") for t in range(TILES)]
+
+        def interleaved(g, c0, c1):
+            return h_raw[g][:, :, c0:c1].rearrange("p j w -> p w j")
+
+        def quantise(grouped, codes, scales):
+            nc.vector.quantize_mx(out=codes[:].bitcast(FP8X4), scales=scales[:], in_=grouped[:].rearrange("p w j -> p (w j)"))
+
+        def multiply(g, t, keys, codes, scales):
+            nc.tensor.matmul_mx(
+                out=acc[t][:],
+                lhsT=codes.bitcast(FP8X4),
+                lhsT_scale=scales,
+                rhs=keys[:].bitcast(FP8X4),
+                rhs_scale=key_scales[4 * g : P, :],
+                start=(g == 0),
+                stop=(g == PASSES - 1),
+            )
+
+        keys0 = keep.tile([P, S], U32, name="keys0", align_bytes=64)
+        nc.vector.tensor_copy(keys0[:], word_table[0][:].bitcast(U32).indirect(offsets[:]))
+        nc.vector.tensor_copy(key_scales[:], scale_table[:].indirect(offsets[:]))
+        grouped0 = keep.tile([P, V, PACK], BF16, name="grouped0", tag="chain_b", align_bytes=64)
+        codes0 = keep.tile([P, V], U32, name="codes0", tag="chain_a", align_bytes=64)
+        scales0 = keep.tile([P, V], U8, name="scales0", align_bytes=64)
+        nc.scalar.activation(grouped0[:], interleaved(0, 0, V), ACT.Copy)
+        quantise(grouped0, codes0, scales0)
+        for t in range(TILES):
+            multiply(0, t, keys0, codes0[:, t * P : (t + 1) * P], scales0[:, t * P : (t + 1) * P])
+
+        keys1 = keep.tile([P, S], U32, name="keys1", tag="chain_b", align_bytes=64)
+        nc.vector.tensor_copy(keys1[:], word_table[1][:].bitcast(U32).indirect(offsets[:]))
+        grouped1 = keep.tile([P, P, PACK], BF16, name="grouped1", tag="chain_c", align_bytes=64)
+        grouped2 = keep.tile([P, P, PACK], BF16, name="grouped2", align_bytes=64)
+        nc.vector.tensor_copy(grouped1[:], interleaved(1, 0, P))
+        nc.scalar.activation(grouped2[:], interleaved(1, P, V), ACT.Copy)
+        codes1 = keep.tile([P, P], U32, name="codes1", align_bytes=64)
+        scales1 = keep.tile([P, P], U8, name="scales1", align_bytes=64)
+        quantise(grouped1, codes1, scales1)
+        multiply(1, 0, keys1, codes1[:], scales1[:])
+        codes2 = keep.tile([P, P], U32, name="codes2", tag="chain_c", align_bytes=64)
+        scales2 = keep.tile([P, P], U8, name="scales2", align_bytes=64)
+        quantise(grouped2, codes2, scales2)
+        multiply(1, 1, keys1, codes2[:], scales2[:])
+
+        H = S // 2
+        halves = [slice(0, H), slice(H, S)]
+
+        def small(name, n=1):
+            return [keep.tile([P, n], F32, name=f"{name}{t}") for t in range(TILES)]
+
+        def wide(name):
+            return [keep.tile([P, S], F32, name=f"{name}{t}", align_bytes=64) for t in range(TILES)]
+
+        neg_max, part_total, total, inv, coef = small("neg_max"), small("part_total", 2), small("total"), small("inv"), small("coef", 4)
+        sum_a, sum_b, bias_a, bias = small("sum_a"), small("sum_b"), small("bias_a"), small("bias")
+        pair, pooled, half_p, th, kept, res = wide("pair"), wide("pooled"), wide("half_p"), wide("th"), wide("kept"), wide("res")
+
+        def shifted(t, cols, by):
+            return e[t][:, PAD + by + cols.start : PAD + by + cols.stop]
+
+        def row_max(t):
+            nc.vector.tensor_reduce(neg_max[t][:], acc[t][:], AX.X, ALU.max, negate=True)
+
+        def exponentials(t):
+            for h, cols in enumerate(halves):
+                nc.scalar.activation(shifted(t, cols, 0), acc[t][:, cols], ACT.Exp, bias=neg_max[t][:], scale=1.0, accum_out=part_total[t][:, h : h + 1])
+            nc.scalar.activation(total[t][:], part_total[t][:, 0:1], ACT.Identity, bias=part_total[t][:, 1:2], scale=1.0)
+
+        def pool(t):
+            for cols in halves:
+                nc.vector.tensor_tensor(pair[t][:, cols], shifted(t, cols, -1), shifted(t, cols, 0), ALU.max)
+            nc.vector.reciprocal(inv[t][:], total[t][:])
+            for cols, s in zip(halves, (sum_a, sum_b)):
+                nc.vector.scalar_tensor_tensor(pooled[t][:, cols], pair[t][:, cols], 1.0, shifted(t, cols, 1), ALU.mult, ALU.max, accum_out=s[t][:])
+
+        def gate(t):
+            nc.scalar.activation(coef[t][:], consts[:], ACT.Copy, scale=inv[t][:])
+            nc.scalar.activation(bias_a[t][:], sum_a[t][:], ACT.Copy, scale=coef[t][:, 2:3])
+            nc.scalar.activation(half_p[t][:], e[t][:, PAD : PAD + S], ACT.Copy, scale=coef[t][:, 0:1])
+            nc.scalar.activation(bias[t][:], sum_b[t][:], ACT.Identity, bias=bias_a[t][:], scale=coef[t][:, 2:3])
+            for cols in halves:
+                nc.scalar.activation(th[t][:, cols], pooled[t][:, cols], ACT.Tanh, bias=bias[t][:], scale=coef[t][:, 1:2])
+
+        def finish(t):
+            for cols in halves:
+                nc.vector.scalar_tensor_tensor(kept[t][:, cols], th[t][:, cols], 1.0, half_p[t][:, cols], ALU.add, ALU.mult)
+            for cols in halves:
+                nc.vector.scalar_tensor_tensor(res[t][:, cols], pooled[t][:, cols], coef[t][:, 3:4], kept[t][:, cols], ALU.mult, ALU.add)
+                nc.sync.dma_start(out[t * P : (t + 1) * P, cols], res[t][:, cols])
+
+        for step in (row_max, exponentials, pool, gate, finish):
+            for t in range(TILES):
+                step(t)

@@ -31,24 +31,21 @@ def tile_picked_ysnapv_max_p_kernel(tc, x_words, x_scales, hT, offs, out):
         psum = ctx.enter_context(tc.psum_pool(name="psum", bufs=1))
 
         offsets = keep.tile([P, S // 16], U16, name="offsets")
-        scale_table = keep.tile([P, T], U8, name="scale_table", tag="chain_a", align_bytes=64)
-        nc.vector.memset(scale_table[:].bitcast(I32), 0)
-        for q in range(4):
-            nc.scalar.dma_start(
-                scale_table[32 * q : 32 * q + 4 * PASSES, :].bitcast(I32),
-                x_scales[:, 4 * q : 4 * q + 4, :].bitcast(I32),
-            )
-
+        nc.sync.dma_start(offsets[:], offs)
+        h_raw = keep.tile([P, PASSES, PACK, V], F32, name="h_raw", tag="chain_b", align_bytes=64)
+        nc.sync.dma_start(h_raw[:], hT.rearrange("(g p j) w -> p g j w", g=PASSES, j=PACK))
         word_table = [
-            keep.tile([P, T], I32, name="word_table0", align_bytes=64),
-            keep.tile([P, T], I32, name="word_table1", tag="chain_c", align_bytes=64),
+            keep.tile([P, T], I32, name="word_table0", tag="chain_c", align_bytes=64),
+            keep.tile([P, T], I32, name="word_table1", align_bytes=64),
         ]
-        h_raw = [keep.tile([P, PACK, V], F32, name=f"h_raw{g}", align_bytes=64) for g in range(PASSES)]
         for g in range(PASSES):
             nc.sync.dma_start(word_table[g][:], x_words[g].rearrange("p n t -> p (n t)").bitcast(I32))
-            if g == 0:
-                nc.sync.dma_start(offsets[:], offs)
-            nc.sync.dma_start(h_raw[g][:], hT[g * K_PASS : (g + 1) * K_PASS, :].rearrange("(p j) w -> p j w", j=PACK))
+
+        scale_table = keep.tile([P, T], U8, name="scale_table", tag="chain_a", align_bytes=64)
+        nc.gpsimd.memset(scale_table[:].bitcast(I32), 0)
+        nc.scalar.dma_start(scale_table[0:P:4, :].bitcast(I32), x_scales.rearrange("g r n -> (g r) n").bitcast(I32))
+        key_scales = keep.tile([P, PASSES * S], U8, name="key_scales", align_bytes=64)
+        nc.gpsimd.memset(key_scales[:].bitcast(I32), 0)
 
         consts = keep.tile([P, 4], F32, name="consts")
         for i, c in enumerate((50.0, 200.0, -300.0 / S, 20.0)):
@@ -58,51 +55,39 @@ def tile_picked_ysnapv_max_p_kernel(tc, x_words, x_scales, hT, offs, out):
             nc.vector.memset(e[t][:, PAD - 1 : PAD], 0.0)
             nc.vector.memset(e[t][:, PAD + S : PAD + S + 1], 0.0)
 
-        key_scales = keep.tile([P, S], U8, name="key_scales", align_bytes=64)
+        picked_scales = keep.tile([P, S], U8, name="picked_scales", align_bytes=64)
+        nc.vector.tensor_copy(picked_scales[:], scale_table[:].indirect(offsets[:]))
+        for g in range(PASSES):
+            for q in range(4):
+                src = 64 * g + 16 * q
+                queue = nc.gpsimd if (g == 1 and q >= 2) else nc.scalar
+                queue.dma_start(
+                    key_scales[32 * q : 32 * q + 4, g * S : (g + 1) * S].bitcast(I32),
+                    picked_scales[src : src + 16 : 4, :].bitcast(I32),
+                )
+
+        grouped = keep.tile([P, PASSES, V, PACK], BF16, name="grouped", tag="chain_a", align_bytes=64)
+        codes = [keep.tile([P, V], U32, name=f"codes{g}", align_bytes=64) for g in range(PASSES)]
+        scales = [keep.tile([P, V], U8, name=f"scales{g}", align_bytes=64) for g in range(PASSES)]
+        for g in range(PASSES):
+            nc.vector.tensor_copy(grouped[:, g], h_raw[:, g].rearrange("p j w -> p w j"))
+        for g in range(PASSES):
+            nc.vector.quantize_mx(out=codes[g][:].bitcast(FP8X4), scales=scales[g][:], in_=grouped[:, g].rearrange("p w j -> p (w j)"))
+
         acc = [psum.tile([P, S], F32, name=f"acc{t}") for t in range(TILES)]
-
-        def interleaved(g, c0, c1):
-            return h_raw[g][:, :, c0:c1].rearrange("p j w -> p w j")
-
-        def quantise(grouped, codes, scales):
-            nc.vector.quantize_mx(out=codes[:].bitcast(FP8X4), scales=scales[:], in_=grouped[:].rearrange("p w j -> p (w j)"))
-
-        def multiply(g, t, keys, codes, scales):
-            nc.tensor.matmul_mx(
-                out=acc[t][:],
-                lhsT=codes.bitcast(FP8X4),
-                lhsT_scale=scales,
-                rhs=keys[:].bitcast(FP8X4),
-                rhs_scale=key_scales[4 * g : P, :],
-                start=(g == 0),
-                stop=(g == PASSES - 1),
-            )
-
-        keys0 = keep.tile([P, S], U32, name="keys0", align_bytes=64)
-        nc.vector.tensor_copy(keys0[:], word_table[0][:].bitcast(U32).indirect(offsets[:]))
-        nc.vector.tensor_copy(key_scales[:], scale_table[:].indirect(offsets[:]))
-        grouped0 = keep.tile([P, V, PACK], BF16, name="grouped0", tag="chain_b", align_bytes=64)
-        codes0 = keep.tile([P, V], U32, name="codes0", tag="chain_a", align_bytes=64)
-        scales0 = keep.tile([P, V], U8, name="scales0", align_bytes=64)
-        nc.scalar.activation(grouped0[:], interleaved(0, 0, V), ACT.Copy)
-        quantise(grouped0, codes0, scales0)
-        for t in range(TILES):
-            multiply(0, t, keys0, codes0[:, t * P : (t + 1) * P], scales0[:, t * P : (t + 1) * P])
-
-        keys1 = keep.tile([P, S], U32, name="keys1", tag="chain_b", align_bytes=64)
-        nc.vector.tensor_copy(keys1[:], word_table[1][:].bitcast(U32).indirect(offsets[:]))
-        grouped1 = keep.tile([P, P, PACK], BF16, name="grouped1", tag="chain_c", align_bytes=64)
-        grouped2 = keep.tile([P, P, PACK], BF16, name="grouped2", align_bytes=64)
-        nc.vector.tensor_copy(grouped1[:], interleaved(1, 0, P))
-        nc.scalar.activation(grouped2[:], interleaved(1, P, V), ACT.Copy)
-        codes1 = keep.tile([P, P], U32, name="codes1", align_bytes=64)
-        scales1 = keep.tile([P, P], U8, name="scales1", align_bytes=64)
-        quantise(grouped1, codes1, scales1)
-        multiply(1, 0, keys1, codes1[:], scales1[:])
-        codes2 = keep.tile([P, P], U32, name="codes2", tag="chain_c", align_bytes=64)
-        scales2 = keep.tile([P, P], U8, name="scales2", align_bytes=64)
-        quantise(grouped2, codes2, scales2)
-        multiply(1, 1, keys1, codes2[:], scales2[:])
+        for g in range(PASSES):
+            keys = keep.tile([P, S], U32, name=f"keys{g}", tag=("chain_b", "chain_c")[g], align_bytes=64)
+            nc.vector.tensor_copy(keys[:], word_table[g][:].bitcast(U32).indirect(offsets[:]))
+            for t in range(TILES):
+                nc.tensor.matmul_mx(
+                    out=acc[t][:],
+                    lhsT=codes[g][:, t * P : (t + 1) * P].bitcast(FP8X4),
+                    lhsT_scale=scales[g][:, t * P : (t + 1) * P],
+                    rhs=keys[:].bitcast(FP8X4),
+                    rhs_scale=key_scales[:, g * S : (g + 1) * S],
+                    start=(g == 0),
+                    stop=(g == PASSES - 1),
+                )
 
         H = S // 2
         halves = [slice(0, H), slice(H, S)]
@@ -113,9 +98,11 @@ def tile_picked_ysnapv_max_p_kernel(tc, x_words, x_scales, hT, offs, out):
         def wide(name):
             return [keep.tile([P, S], F32, name=f"{name}{t}", align_bytes=64) for t in range(TILES)]
 
-        neg_max, part_total, total, inv, coef = small("neg_max"), small("part_total", 2), small("total"), small("inv"), small("coef", 4)
-        sum_a, sum_b, bias_a, bias = small("sum_a"), small("sum_b"), small("bias_a"), small("bias")
-        pair, pooled, half_p, th, kept, res = wide("pair"), wide("pooled"), wide("half_p"), wide("th"), wide("kept"), wide("res")
+        neg_max, total, inv, coef = small("neg_max"), small("total"), small("inv"), small("coef", 4)
+        sum_a, sum_b, bias = small("sum_a"), small("sum_b"), small("bias")
+        pooled, half_p, th, kept, res = wide("pooled"), wide("half_p"), wide("th"), wide("kept"), wide("res")
+
+        pair = keep.tile([P, S], F32, name="pair", align_bytes=64)
 
         def shifted(t, cols, by):
             return e[t][:, PAD + by + cols.start : PAD + by + cols.stop]
@@ -124,22 +111,20 @@ def tile_picked_ysnapv_max_p_kernel(tc, x_words, x_scales, hT, offs, out):
             nc.vector.tensor_reduce(neg_max[t][:], acc[t][:], AX.X, ALU.max, negate=True)
 
         def exponentials(t):
-            for h, cols in enumerate(halves):
-                nc.scalar.activation(shifted(t, cols, 0), acc[t][:, cols], ACT.Exp, bias=neg_max[t][:], scale=1.0, accum_out=part_total[t][:, h : h + 1])
-            nc.scalar.activation(total[t][:], part_total[t][:, 0:1], ACT.Identity, bias=part_total[t][:, 1:2], scale=1.0)
+            nc.scalar.activation(e[t][:, PAD : PAD + S], acc[t][:], ACT.Exp, bias=neg_max[t][:], scale=1.0, accum_out=total[t][:])
 
         def pool(t):
             for cols in halves:
-                nc.vector.tensor_tensor(pair[t][:, cols], shifted(t, cols, -1), shifted(t, cols, 0), ALU.max)
+                nc.vector.tensor_tensor(pair[:, cols], shifted(t, cols, -1), shifted(t, cols, 0), ALU.max)
             nc.vector.reciprocal(inv[t][:], total[t][:])
             for cols, s in zip(halves, (sum_a, sum_b)):
-                nc.vector.scalar_tensor_tensor(pooled[t][:, cols], pair[t][:, cols], 1.0, shifted(t, cols, 1), ALU.mult, ALU.max, accum_out=s[t][:])
+                nc.vector.scalar_tensor_tensor(pooled[t][:, cols], pair[:, cols], 1.0, shifted(t, cols, 1), ALU.mult, ALU.max, accum_out=s[t][:])
 
         def gate(t):
             nc.scalar.activation(coef[t][:], consts[:], ACT.Copy, scale=inv[t][:])
-            nc.scalar.activation(bias_a[t][:], sum_a[t][:], ACT.Copy, scale=coef[t][:, 2:3])
-            nc.scalar.activation(half_p[t][:], e[t][:, PAD : PAD + S], ACT.Copy, scale=coef[t][:, 0:1])
-            nc.scalar.activation(bias[t][:], sum_b[t][:], ACT.Identity, bias=bias_a[t][:], scale=coef[t][:, 2:3])
+            nc.scalar.activation(half_p[t][:, halves[0]], shifted(t, halves[0], 0), ACT.Copy, scale=coef[t][:, 0:1])
+            nc.vector.scalar_tensor_tensor(bias[t][:], sum_a[t][:], sum_b[t][:], coef[t][:, 2:3], ALU.add, ALU.mult)
+            nc.scalar.activation(half_p[t][:, halves[1]], shifted(t, halves[1], 0), ACT.Copy, scale=coef[t][:, 0:1])
             for cols in halves:
                 nc.scalar.activation(th[t][:, cols], pooled[t][:, cols], ACT.Tanh, bias=bias[t][:], scale=coef[t][:, 1:2])
 
@@ -150,6 +135,11 @@ def tile_picked_ysnapv_max_p_kernel(tc, x_words, x_scales, hT, offs, out):
                 nc.vector.scalar_tensor_tensor(res[t][:, cols], pooled[t][:, cols], coef[t][:, 3:4], kept[t][:, cols], ALU.mult, ALU.add)
                 nc.sync.dma_start(out[t * P : (t + 1) * P, cols], res[t][:, cols])
 
-        for step in (row_max, exponentials, pool, gate, finish):
+        for step in (row_max, exponentials):
             for t in range(TILES):
                 step(t)
+        for t in range(TILES):
+            pool(t)
+            gate(t)
+        for t in range(TILES):
+            finish(t)

@@ -22,6 +22,8 @@ K_PASS = P * PACK
 PASSES = K // K_PASS
 TILES = V // P
 PAD = 4
+ROW0 = 12
+SCALE_START = (12, 0)
 
 
 def tile_picked_ysnapv_max_p_kernel(tc, x_words, x_scales, hT, offs, out):
@@ -43,9 +45,7 @@ def tile_picked_ysnapv_max_p_kernel(tc, x_words, x_scales, hT, offs, out):
 
         scale_table = keep.tile([P, T], U8, name="scale_table", tag="chain_a", align_bytes=64)
         nc.gpsimd.memset(scale_table[:].bitcast(I32), 0)
-        nc.scalar.dma_start(scale_table[0:P:4, :].bitcast(I32), x_scales.rearrange("g r n -> (g r) n").bitcast(I32))
-        key_scales = keep.tile([P, PASSES * S], U8, name="key_scales", align_bytes=64)
-        nc.gpsimd.memset(key_scales[:].bitcast(I32), 0)
+        nc.scalar.dma_start(scale_table[ROW0 : ROW0 + 32, :].bitcast(I32), x_scales.rearrange("g r n -> (g r) n").bitcast(I32))
 
         consts = keep.tile([P, 4], F32, name="consts")
         for i, c in enumerate((50.0, 200.0, -300.0 / S, 20.0)):
@@ -57,22 +57,27 @@ def tile_picked_ysnapv_max_p_kernel(tc, x_words, x_scales, hT, offs, out):
 
         picked_scales = keep.tile([P, S], U8, name="picked_scales", align_bytes=64)
         nc.vector.tensor_copy(picked_scales[:], scale_table[:].indirect(offsets[:]))
+        key_scales = [keep.tile([P, S], U8, name=f"key_scales{g}", align_bytes=64) for g in range(PASSES)]
+        for g in range(PASSES):
+            nc.vector.tensor_copy(key_scales[g][:].bitcast(I32), picked_scales[:].bitcast(I32))
         for g in range(PASSES):
             for q in range(4):
-                src = 64 * g + 16 * q
-                queue = nc.gpsimd if (g == 1 and q >= 2) else nc.scalar
-                queue.dma_start(
-                    key_scales[32 * q : 32 * q + 4, g * S : (g + 1) * S].bitcast(I32),
-                    picked_scales[src : src + 16 : 4, :].bitcast(I32),
-                )
+                src = ROW0 + 16 * g + 4 * q
+                dst = 32 * q + SCALE_START[g]
+                if src != dst:
+                    nc.scalar.dma_start(key_scales[g][dst : dst + 4, :].bitcast(I32), picked_scales[src : src + 4, :].bitcast(I32))
 
-        grouped = keep.tile([P, PASSES, V, PACK], BF16, name="grouped", tag="chain_a", align_bytes=64)
-        codes = [keep.tile([P, V], U32, name=f"codes{g}", align_bytes=64) for g in range(PASSES)]
-        scales = [keep.tile([P, V], U8, name=f"scales{g}", align_bytes=64) for g in range(PASSES)]
+        grouped = [
+            keep.tile([P, V, PACK], BF16, name="grouped0", tag="chain_a", align_bytes=64),
+            keep.tile([P, V, PACK], BF16, name="grouped1", align_bytes=64),
+        ]
+        nc.vector.tensor_copy(grouped[0][:], h_raw[:, 0].rearrange("p j w -> p w j"))
+        nc.scalar.activation(grouped[1][:], h_raw[:, 1].rearrange("p j w -> p w j"), ACT.Copy)
+        codes, scales = [], []
         for g in range(PASSES):
-            nc.vector.tensor_copy(grouped[:, g], h_raw[:, g].rearrange("p j w -> p w j"))
-        for g in range(PASSES):
-            nc.vector.quantize_mx(out=codes[g][:].bitcast(FP8X4), scales=scales[g][:], in_=grouped[:, g].rearrange("p w j -> p (w j)"))
+            codes.append(keep.tile([P, V], U32, name=f"codes{g}", tag=("codes0", "chain_a")[g], align_bytes=64))
+            scales.append(keep.tile([P, V], U8, name=f"scales{g}", align_bytes=64))
+            nc.vector.quantize_mx(out=codes[g][:].bitcast(FP8X4), scales=scales[g][:], in_=grouped[g][:].rearrange("p w j -> p (w j)"))
 
         acc = [psum.tile([P, S], F32, name=f"acc{t}") for t in range(TILES)]
         for g in range(PASSES):
@@ -84,7 +89,7 @@ def tile_picked_ysnapv_max_p_kernel(tc, x_words, x_scales, hT, offs, out):
                     lhsT=codes[g][:, t * P : (t + 1) * P].bitcast(FP8X4),
                     lhsT_scale=scales[g][:, t * P : (t + 1) * P],
                     rhs=keys[:].bitcast(FP8X4),
-                    rhs_scale=key_scales[:, g * S : (g + 1) * S],
+                    rhs_scale=key_scales[g][SCALE_START[g] : P, :],
                     start=(g == 0),
                     stop=(g == PASSES - 1),
                 )

@@ -34,10 +34,10 @@ def tile_picked_ysnapv_max_p_kernel(tc, x_words, x_scales, hT, offs, out):
 
         offsets = keep.tile([P, S // 16], U16, name="offsets")
         nc.sync.dma_start(offsets[:], offs)
-        h_raw = keep.tile([P, PASSES, PACK, V], F32, name="h_raw", tag="chain_b", align_bytes=64)
+        h_raw = keep.tile([P, PASSES, PACK, V], F32, name="h_raw", align_bytes=64)
         nc.sync.dma_start(h_raw[:], hT.rearrange("(g p j) w -> p g j w", g=PASSES, j=PACK))
         word_table = [
-            keep.tile([P, T], I32, name="word_table0", tag="chain_c", align_bytes=64),
+            keep.tile([P, T], I32, name="word_table0", tag="chain_b", align_bytes=64),
             keep.tile([P, T], I32, name="word_table1", align_bytes=64),
         ]
         for g in range(PASSES):
@@ -47,9 +47,11 @@ def tile_picked_ysnapv_max_p_kernel(tc, x_words, x_scales, hT, offs, out):
         nc.gpsimd.memset(scale_table[:].bitcast(I32), 0)
         nc.scalar.dma_start(scale_table[ROW0 : ROW0 + 32, :].bitcast(I32), x_scales.rearrange("g r n -> (g r) n").bitcast(I32))
 
+        tenths = keep.tile([P, 4], F32, name="tenths")
+        for i, c in enumerate((5.0, 20.0, -30.0 / S, 2.0)):
+            nc.gpsimd.memset(tenths[:, i : i + 1], c)
         consts = keep.tile([P, 4], F32, name="consts")
-        for i, c in enumerate((50.0, 200.0, -300.0 / S, 20.0)):
-            nc.vector.memset(consts[:, i : i + 1], c)
+        nc.scalar.activation(consts[:], tenths[:], ACT.Copy, scale=10.0)
         e = [keep.tile([P, S + 2 * PAD], F32, name=f"e{t}", align_bytes=64) for t in range(TILES)]
         for t in range(TILES):
             nc.vector.memset(e[t][:, PAD - 1 : PAD], 0.0)
@@ -60,42 +62,41 @@ def tile_picked_ysnapv_max_p_kernel(tc, x_words, x_scales, hT, offs, out):
         key_scales = [keep.tile([P, S], U8, name=f"key_scales{g}", align_bytes=64) for g in range(PASSES)]
         for g in range(PASSES):
             nc.vector.tensor_copy(key_scales[g][:].bitcast(I32), picked_scales[:].bitcast(I32))
-        for g in range(PASSES):
+        for g, queue in enumerate((nc.scalar, nc.sync)):
             for q in range(4):
                 src = ROW0 + 16 * g + 4 * q
                 dst = 32 * q + SCALE_START[g]
                 if src != dst:
-                    nc.scalar.dma_start(key_scales[g][dst : dst + 4, :].bitcast(I32), picked_scales[src : src + 4, :].bitcast(I32))
+                    queue.dma_start(key_scales[g][dst : dst + 4, :].bitcast(I32), picked_scales[src : src + 4, :].bitcast(I32))
 
         grouped = [
             keep.tile([P, V, PACK], BF16, name="grouped0", tag="chain_a", align_bytes=64),
-            keep.tile([P, V, PACK], BF16, name="grouped1", align_bytes=64),
+            keep.tile([P, V, PACK], BF16, name="grouped1", tag="chain_c", align_bytes=64),
         ]
         nc.vector.tensor_copy(grouped[0][:], h_raw[:, 0].rearrange("p j w -> p w j"))
-        nc.scalar.activation(grouped[1][:], h_raw[:, 1].rearrange("p j w -> p w j"), ACT.Copy)
-        codes, scales = [], []
-        for g in range(PASSES):
-            codes.append(keep.tile([P, V], U32, name=f"codes{g}", tag=("codes0", "chain_a")[g], align_bytes=64))
-            scales.append(keep.tile([P, V], U8, name=f"scales{g}", align_bytes=64))
-            nc.vector.quantize_mx(out=codes[g][:].bitcast(FP8X4), scales=scales[g][:], in_=grouped[g][:].rearrange("p w j -> p (w j)"))
-
-        acc = [psum.tile([P, S], F32, name=f"acc{t}") for t in range(TILES)]
-        for g in range(PASSES):
-            keys = keep.tile([P, S], U32, name=f"keys{g}", tag=("chain_b", "chain_c")[g], align_bytes=64)
-            nc.vector.tensor_copy(keys[:], word_table[g][:].bitcast(U32).indirect(offsets[:]))
-            for t in range(TILES):
-                nc.tensor.matmul_mx(
-                    out=acc[t][:],
-                    lhsT=codes[g][:, t * P : (t + 1) * P].bitcast(FP8X4),
-                    lhsT_scale=scales[g][:, t * P : (t + 1) * P],
-                    rhs=keys[:].bitcast(FP8X4),
-                    rhs_scale=key_scales[g][SCALE_START[g] : P, :],
-                    start=(g == 0),
-                    stop=(g == PASSES - 1),
-                )
+        nc.scalar.copy(grouped[1][:], h_raw[:, 1].rearrange("p j w -> p w j"))
 
         H = S // 2
         halves = [slice(0, H), slice(H, S)]
+        acc = [[psum.tile([P, H], F32, name=f"acc{t}_{h}") for h in range(2)] for t in range(TILES)]
+        for g in range(PASSES):
+            codes = keep.tile([P, V], U32, name=f"codes{g}", tag=("codes0", "chain_b")[g], align_bytes=64)
+            scales = keep.tile([P, V], U8, name=f"scales{g}", align_bytes=64)
+            nc.vector.quantize_mx(out=codes[:].bitcast(FP8X4), scales=scales[:], in_=grouped[g][:].rearrange("p w j -> p (w j)"))
+            keys = keep.tile([P, S], U32, name=f"keys{g}", tag=("chain_a", "chain_c")[g], align_bytes=64)
+            for h, cols in enumerate(halves):
+                nc.vector.tensor_copy(keys[:, cols], word_table[g][:].bitcast(U32).indirect(offsets[:, cols.start // 16 : cols.stop // 16]))
+                for t in range(TILES):
+                    nc.tensor.matmul_mx(
+                        out=acc[t][h][:],
+                        lhsT=codes[:, t * P : (t + 1) * P].bitcast(FP8X4),
+                        lhsT_scale=scales[:, t * P : (t + 1) * P],
+                        rhs=keys[:, cols].bitcast(FP8X4),
+                        rhs_scale=key_scales[g][SCALE_START[g] : P, cols],
+                        start=(g == 0),
+                        stop=(g == PASSES - 1),
+                    )
+
 
         def small(name, n=1):
             return [keep.tile([P, n], F32, name=f"{name}{t}") for t in range(TILES)]
@@ -112,11 +113,14 @@ def tile_picked_ysnapv_max_p_kernel(tc, x_words, x_scales, hT, offs, out):
         def shifted(t, cols, by):
             return e[t][:, PAD + by + cols.start : PAD + by + cols.stop]
 
-        def row_max(t):
-            nc.vector.tensor_reduce(neg_max[t][:], acc[t][:], AX.X, ALU.max, negate=True)
+        neg_y, part_max = wide("neg_y"), small("part_max")
+
+        def row_max(t, h):
+            first, low = ((None, part_max[t]), (part_max[t][:], neg_max[t]))[h]
+            nc.vector.tensor_scalar(neg_y[t][:, halves[h]], acc[t][h][:], -1.0, first, ALU.mult, ALU.min, accum_out=low[:])
 
         def exponentials(t):
-            nc.scalar.activation(e[t][:, PAD : PAD + S], acc[t][:], ACT.Exp, bias=neg_max[t][:], scale=1.0, accum_out=total[t][:])
+            nc.scalar.activation(e[t][:, PAD : PAD + S], neg_y[t][:], ACT.Exp, bias=neg_max[t][:], scale=-1.0, accum_out=total[t][:])
 
         def pool(t):
             for cols in halves:
@@ -140,9 +144,11 @@ def tile_picked_ysnapv_max_p_kernel(tc, x_words, x_scales, hT, offs, out):
                 nc.vector.scalar_tensor_tensor(res[t][:, cols], pooled[t][:, cols], coef[t][:, 3:4], kept[t][:, cols], ALU.mult, ALU.add)
                 nc.sync.dma_start(out[t * P : (t + 1) * P, cols], res[t][:, cols])
 
-        for step in (row_max, exponentials):
+        for h in range(2):
             for t in range(TILES):
-                step(t)
+                row_max(t, h)
+        for t in range(TILES):
+            exponentials(t)
         for t in range(TILES):
             pool(t)
             gate(t)

@@ -36,22 +36,21 @@ def tile_picked_ysnapv_max_p_kernel(tc, x_words, x_scales, hT, offs, out):
         nc.sync.dma_start(offsets[:], offs)
         h_raw = keep.tile([P, PASSES, PACK, V], F32, name="h_raw", align_bytes=64)
         nc.sync.dma_start(h_raw[:], hT.rearrange("(g p j) w -> p g j w", g=PASSES, j=PACK))
-        word_table = [
-            keep.tile([P, T], I32, name="word_table0", tag="chain_b", align_bytes=64),
-            keep.tile([P, T], I32, name="word_table1", align_bytes=64),
-        ]
-        for g in range(PASSES):
-            nc.sync.dma_start(word_table[g][:], x_words[g].rearrange("p n t -> p (n t)").bitcast(I32))
 
         scale_table = keep.tile([P, T], U8, name="scale_table", tag="chain_a", align_bytes=64)
         nc.gpsimd.memset(scale_table[:].bitcast(I32), 0)
-        nc.scalar.dma_start(scale_table[ROW0 : ROW0 + 32, :].bitcast(I32), x_scales.rearrange("g r n -> (g r) n").bitcast(I32))
+        nc.sync.dma_start(scale_table[ROW0 : ROW0 + 32, :].bitcast(I32), x_scales.rearrange("g r n -> (g r) n").bitcast(I32))
 
-        tenths = keep.tile([P, 4], F32, name="tenths")
+        tenths = keep.tile([P, 4], F32, name="tenths", tag="chain_b", align_bytes=64)
         for i, c in enumerate((5.0, 20.0, -30.0 / S, 2.0)):
             nc.gpsimd.memset(tenths[:, i : i + 1], c)
         consts = keep.tile([P, 4], F32, name="consts")
-        nc.scalar.activation(consts[:], tenths[:], ACT.Copy, scale=10.0)
+        nc.gpsimd.tensor_scalar(consts[:], tenths[:], 10.0, 0.0, ALU.mult, ALU.add)
+
+        word_table = keep.tile([P, PASSES * T], I32, name="word_table", tag="chain_b", align_bytes=64)
+        for g in range(PASSES):
+            nc.sync.dma_start(word_table[:, g * T : (g + 1) * T], x_words[g].rearrange("p n t -> p (n t)").bitcast(I32))
+
         e = [keep.tile([P, S + 2 * PAD], F32, name=f"e{t}", align_bytes=64) for t in range(TILES)]
         for t in range(TILES):
             nc.vector.memset(e[t][:, PAD - 1 : PAD], 0.0)
@@ -62,12 +61,12 @@ def tile_picked_ysnapv_max_p_kernel(tc, x_words, x_scales, hT, offs, out):
         key_scales = [keep.tile([P, S], U8, name=f"key_scales{g}", align_bytes=64) for g in range(PASSES)]
         for g in range(PASSES):
             nc.vector.tensor_copy(key_scales[g][:].bitcast(I32), picked_scales[:].bitcast(I32))
-        for g, queue in enumerate((nc.scalar, nc.sync)):
+        for g in range(PASSES):
             for q in range(4):
                 src = ROW0 + 16 * g + 4 * q
                 dst = 32 * q + SCALE_START[g]
                 if src != dst:
-                    queue.dma_start(key_scales[g][dst : dst + 4, :].bitcast(I32), picked_scales[src : src + 4, :].bitcast(I32))
+                    nc.scalar.dma_start(key_scales[g][dst : dst + 4, :].bitcast(I32), picked_scales[src : src + 4, :].bitcast(I32))
 
         grouped = [
             keep.tile([P, V, PACK], BF16, name="grouped0", tag="chain_a", align_bytes=64),
@@ -80,12 +79,12 @@ def tile_picked_ysnapv_max_p_kernel(tc, x_words, x_scales, hT, offs, out):
         halves = [slice(0, H), slice(H, S)]
         acc = [[psum.tile([P, H], F32, name=f"acc{t}_{h}") for h in range(2)] for t in range(TILES)]
         for g in range(PASSES):
-            codes = keep.tile([P, V], U32, name=f"codes{g}", tag=("codes0", "chain_b")[g], align_bytes=64)
+            codes = keep.tile([P, V], U32, name=f"codes{g}", align_bytes=64)
             scales = keep.tile([P, V], U8, name=f"scales{g}", align_bytes=64)
             nc.vector.quantize_mx(out=codes[:].bitcast(FP8X4), scales=scales[:], in_=grouped[g][:].rearrange("p w j -> p (w j)"))
             keys = keep.tile([P, S], U32, name=f"keys{g}", tag=("chain_a", "chain_c")[g], align_bytes=64)
             for h, cols in enumerate(halves):
-                nc.vector.tensor_copy(keys[:, cols], word_table[g][:].bitcast(U32).indirect(offsets[:, cols.start // 16 : cols.stop // 16]))
+                nc.vector.tensor_copy(keys[:, cols], word_table[:, g * T : (g + 1) * T].bitcast(U32).indirect(offsets[:, cols.start // 16 : cols.stop // 16]))
                 for t in range(TILES):
                     nc.tensor.matmul_mx(
                         out=acc[t][h][:],

from contextlib import ExitStack

import concourse.mybir as mybir

K, T, S, V = 1024, 2048, 512, 256
FLOPS = 2 * K * S * V

F32 = mybir.dt.float32
BF16 = mybir.dt.bfloat16
I32 = mybir.dt.int32
U32 = mybir.dt.uint32
U16 = mybir.dt.uint16
U8 = mybir.dt.uint8
FP8X4 = mybir.dt.float8_e4m3fn_x4
ALU = mybir.AluOpType
ACT = mybir.ActivationFunctionType
AX = mybir.AxisListType

P = 128
PACK = 4
K_PASS = P * PACK
PASSES = K // K_PASS
TILES = V // P
PAD = 4
ROW0 = 12
SCALE_START = (12, 0)


def tile_picked_ysnapv_max_p_kernel(tc, x_words, x_scales, hT, offs, out):
    nc = tc.nc
    with ExitStack() as ctx:
        keep = ctx.enter_context(tc.tile_pool(name="keep", bufs=1))
        psum = ctx.enter_context(tc.psum_pool(name="psum", bufs=1))

        offsets = keep.tile([P, S // 16], U16, name="offsets")
        nc.sync.dma_start(offsets[:], offs)
        h_raw = keep.tile([P, PASSES, PACK, V], F32, name="h_raw", align_bytes=64)
        nc.sync.dma_start(h_raw[:], hT.rearrange("(g p j) w -> p g j w", g=PASSES, j=PACK))

        scale_table = keep.tile([P, T], U8, name="scale_table", tag="chain_a", align_bytes=64)
        nc.gpsimd.memset(scale_table[:].bitcast(I32), 0)
        nc.sync.dma_start(scale_table[ROW0 : ROW0 + 32, :].bitcast(I32), x_scales.rearrange("g r n -> (g r) n").bitcast(I32))

        tenths = keep.tile([P, 4], F32, name="tenths", tag="chain_b", align_bytes=64)
        for i, c in enumerate((5.0, 20.0, -30.0 / S, 2.0)):
            nc.gpsimd.memset(tenths[:, i : i + 1], c)
        consts = keep.tile([P, 4], F32, name="consts")
        nc.gpsimd.tensor_scalar(consts[:], tenths[:], 10.0, 0.0, ALU.mult, ALU.add)

        word_table = keep.tile([P, PASSES * T], I32, name="word_table", tag="chain_b", align_bytes=64)
        for g in range(PASSES):
            nc.sync.dma_start(word_table[:, g * T : (g + 1) * T], x_words[g].rearrange("p n t -> p (n t)").bitcast(I32))

        e = [keep.tile([P, S + 2 * PAD], F32, name=f"e{t}", align_bytes=64) for t in range(TILES)]
        for t in range(TILES):
            nc.vector.memset(e[t][:, PAD - 1 : PAD], 0.0)
            nc.vector.memset(e[t][:, PAD + S : PAD + S + 1], 0.0)

        picked_scales = keep.tile([P, S], U8, name="picked_scales", align_bytes=64)
        nc.vector.tensor_copy(picked_scales[:], scale_table[:].indirect(offsets[:]))
        key_scales = [keep.tile([P, S], U8, name=f"key_scales{g}", align_bytes=64) for g in range(PASSES)]
        for g in range(PASSES):
            nc.vector.tensor_copy(key_scales[g][:].bitcast(I32), picked_scales[:].bitcast(I32))
        for g in range(PASSES):
            for q in range(4):
                src = ROW0 + 16 * g + 4 * q
                dst = 32 * q + SCALE_START[g]
                if src != dst:
                    nc.scalar.dma_start(key_scales[g][dst : dst + 4, :].bitcast(I32), picked_scales[src : src + 4, :].bitcast(I32))

        grouped = [
            keep.tile([P, V, PACK], BF16, name="grouped0", tag="chain_a", align_bytes=64),
            keep.tile([P, V, PACK], BF16, name="grouped1", tag="chain_c", align_bytes=64),
        ]
        nc.vector.tensor_copy(grouped[0][:], h_raw[:, 0].rearrange("p j w -> p w j"))
        nc.scalar.copy(grouped[1][:], h_raw[:, 1].rearrange("p j w -> p w j"))

        H = S // 2
        halves = [slice(0, H), slice(H, S)]
        acc = [[psum.tile([P, H], F32, name=f"acc{t}_{h}") for h in range(2)] for t in range(TILES)]
        for g in range(PASSES):
            codes = keep.tile([P, V], U32, name=f"codes{g}", align_bytes=64)
            scales = keep.tile([P, V], U8, name=f"scales{g}", align_bytes=64)
            nc.vector.quantize_mx(out=codes[:].bitcast(FP8X4), scales=scales[:], in_=grouped[g][:].rearrange("p w j -> p (w j)"))
            keys = keep.tile([P, S], U32, name=f"keys{g}", tag=("chain_a", "chain_c")[g], align_bytes=64)
            for h, cols in enumerate(halves):
                nc.vector.tensor_copy(keys[:, cols], word_table[:, g * T : (g + 1) * T].bitcast(U32).indirect(offsets[:, cols.start // 16 : cols.stop // 16]))
                for t in range(TILES):
                    nc.tensor.matmul_mx(
                        out=acc[t][h][:],
                        lhsT=codes[:, t * P : (t + 1) * P].bitcast(FP8X4),
                        lhsT_scale=scales[:, t * P : (t + 1) * P],
                        rhs=keys[:, cols].bitcast(FP8X4),
                        rhs_scale=key_scales[g][SCALE_START[g] : P, cols],
                        start=(g == 0),
                        stop=(g == PASSES - 1),
                    )


        def small(name, n=1):
            return [keep.tile([P, n], F32, name=f"{name}{t}") for t in range(TILES)]

        def wide(name):
            return [keep.tile([P, S], F32, name=f"{name}{t}", align_bytes=64) for t in range(TILES)]

        neg_max, total, inv, coef = small("neg_max"), small("total"), small("inv"), small("coef", 4)
        sum_a, sum_b, bias = small("sum_a"), small("sum_b"), small("bias")
        pooled, half_p, th, kept, res = wide("pooled"), wide("half_p"), wide("th"), wide("kept"), wide("res")

        pair = keep.tile([P, S], F32, name="pair", align_bytes=64)

        def shifted(t, cols, by):
            return e[t][:, PAD + by + cols.start : PAD + by + cols.stop]

        neg_y, part_max = wide("neg_y"), small("part_max")

        def row_max(t, h):
            first, low = ((None, part_max[t]), (part_max[t][:], neg_max[t]))[h]
            nc.vector.tensor_scalar(neg_y[t][:, halves[h]], acc[t][h][:], -1.0, first, ALU.mult, ALU.min, accum_out=low[:])

        def exponentials(t):
            nc.scalar.activation(e[t][:, PAD : PAD + S], neg_y[t][:], ACT.Exp, bias=neg_max[t][:], scale=-1.0, accum_out=total[t][:])

        def pool(t):
            for cols in halves:
                nc.vector.tensor_tensor(pair[:, cols], shifted(t, cols, -1), shifted(t, cols, 0), ALU.max)
            nc.vector.reciprocal(inv[t][:], total[t][:])
            for cols, s in zip(halves, (sum_a, sum_b)):
                nc.vector.scalar_tensor_tensor(pooled[t][:, cols], pair[:, cols], 1.0, shifted(t, cols, 1), ALU.mult, ALU.max, accum_out=s[t][:])

        def gate(t):
            nc.scalar.activation(coef[t][:], consts[:], ACT.Copy, scale=inv[t][:])
            nc.scalar.activation(half_p[t][:, halves[0]], shifted(t, halves[0], 0), ACT.Copy, scale=coef[t][:, 0:1])
            nc.vector.scalar_tensor_tensor(bias[t][:], sum_a[t][:], sum_b[t][:], coef[t][:, 2:3], ALU.add, ALU.mult)
            nc.scalar.activation(half_p[t][:, halves[1]], shifted(t, halves[1], 0), ACT.Copy, scale=coef[t][:, 0:1])
            for cols in halves:
                nc.scalar.activation(th[t][:, cols], pooled[t][:, cols], ACT.Tanh, bias=bias[t][:], scale=coef[t][:, 1:2])

        def finish(t):
            for cols in halves:
                nc.vector.scalar_tensor_tensor(kept[t][:, cols], th[t][:, cols], 1.0, half_p[t][:, cols], ALU.add, ALU.mult)
            for cols in halves:
                nc.vector.scalar_tensor_tensor(res[t][:, cols], pooled[t][:, cols], coef[t][:, 3:4], kept[t][:, cols], ALU.mult, ALU.add)
                nc.sync.dma_start(out[t * P : (t + 1) * P, cols], res[t][:, cols])

        for h in range(2):
            for t in range(TILES):
                row_max(t, h)
        for t in range(TILES):
            exponentials(t)
        for t in range(TILES):
            pool(t)
            gate(t)
        for t in range(TILES):
            finish(t)
